import numpy as np
import ml_dtypes


def mxq(x, axis, fmt="e4m3"):
    dtype, down = {"e4m3": (ml_dtypes.float8_e4m3fn, 7), "e5m2": (ml_dtypes.float8_e5m2, 14)}[fmt]
    v = np.moveaxis(np.asarray(x, np.float32).astype(ml_dtypes.bfloat16).astype(np.float64), axis, -1)
    blocks = v.reshape(v.shape[:-1] + (-1, 32))
    amax = np.abs(blocks).max(-1, keepdims=True)
    byte = np.maximum(np.where(amax > 0, np.frexp(amax)[1] - 1 + 127, 0) - down, 1)
    scale = np.exp2(byte - 127.0)
    codes = (blocks / scale).astype(np.float32).astype(dtype).astype(np.float64)
    return np.moveaxis((codes * scale).reshape(v.shape), -1, axis)


WIDE = False


def mx_kscale(k):
    if not WIDE:
        return np.ones(k)
    levels = np.array([10, -10, 5, -5, 0])
    if k % 512:
        return np.exp2(np.random.permutation(np.resize(levels, k // 32))).repeat(32)
    a = np.empty((k // 512, 16))
    for p in range(k // 512):
        a[p, :8] = np.random.permutation(np.resize(levels, 8))
        for g in range(8):
            far = levels[np.abs(levels - a[p, g]) >= 10]
            a[p, g + 8] = far[np.random.randint(len(far))]
    return np.exp2(a.ravel()).repeat(32)


def f64(x):
    return np.asarray(x).astype(np.float64)


def striped(idx):
    return np.tile(idx.reshape(-1, 16).T, (8, 1)).astype(np.uint16)


def unstriped(offs):
    return offs[:16].T.reshape(-1).astype(np.int64)


E2M1 = np.array([0.0, 0.5, 1.0, 1.5, 2.0, 3.0, 4.0, 6.0, -0.0, -0.5, -1.0, -1.5, -2.0, -3.0, -4.0, -6.0])


def pack_weight(w, fmt):
    k, n = w.shape
    w = f64(np.asarray(w, np.float32).astype(ml_dtypes.bfloat16)).reshape(k // 32, 32, n)
    amax = np.abs(w).max(1)
    if fmt == "e4m3":
        byte = np.frexp(amax)[1] - 1 + 127 - 7
    else:
        mant, ex = np.frexp(amax / 6.0)
        byte = np.where(mant > 0.5, ex, ex - 1) + 127
    byte = np.clip(np.where(amax > 0, byte, 1), 1, 254)
    scaled = (w * np.exp2(127.0 - byte)[:, None, :]).reshape(k, n).astype(np.float32)
    by_word = np.ascontiguousarray(scaled.reshape(k // 512, 128, 4, n).transpose(0, 1, 3, 2))
    if fmt == "e4m3":
        words = by_word.astype(ml_dtypes.float8_e4m3fn).view(np.uint8)
    else:
        c = by_word.astype(ml_dtypes.float4_e2m1fn).view(np.uint8) & 0xF
        words = (c[..., 0::2] | (c[..., 1::2] << 4)).reshape(k // 512, 128, 2 * n)
    return np.ascontiguousarray(words), np.ascontiguousarray(byte.astype(np.uint8).reshape(k // 512, 16, n))


def unpack_weight(words, scales, fmt):
    g, _, n = scales.shape
    words = np.ascontiguousarray(words).reshape(g, 128, n, -1)
    if fmt == "e4m3":
        vals = words.view(ml_dtypes.float8_e4m3fn).astype(np.float64)
    else:
        nib = np.empty((g, 128, n, 4), np.uint8)
        nib[..., 0::2] = words & 0xF
        nib[..., 1::2] = words >> 4
        vals = E2M1[nib]
    vals = vals * np.repeat(np.exp2(scales.astype(np.float64) - 127.0), 8, axis=1)[..., None]
    return vals.transpose(0, 1, 3, 2).reshape(g * 512, n)


def gelu(v):
    return 0.5 * v * (1.0 + np.tanh(np.sqrt(2.0 / np.pi) * (v + 0.044715 * v**3)))


K, K2, H, N, T, S = 1536, 512, 1024, 640, 4096, 1024


def setup_inputs():
    n = np.random.standard_normal
    s = mx_kscale(K)[:, None]
    s2 = mx_kscale(K2)[:, None]
    u = mx_kscale(H)[:, None]
    d = {}
    d["tab_words"], d["tab_scales"] = pack_weight(n((K, T)) * s, "e4m3")
    d["offs"] = striped(np.random.permutation(T)[:S])
    d["xs_words"], d["xs_scales"] = pack_weight(n((K2, S)) * s2, "e4m3")
    d["wa"] = (n((K, H)) / K**0.5 / s * u.T).astype(np.float32)
    d["wb"] = (n((K2, H)) / K2**0.5 / s2 * u.T).astype(np.float32)
    d["w2" + "_words"], d["w2" + "_scales"] = pack_weight(n((H, N)) / H**0.5 / u, "e2m1")
    d["wc_words"], d["wc_scales"] = pack_weight(1.4 * n((K2, N)) / K2**0.5 / s2, "e4m3")
    return d


def reference(tab_words, tab_scales, offs, xs_words, xs_scales, wa, wb,
              w2_words, w2_scales, wc_words, wc_scales):
    v = unpack_weight(tab_words, tab_scales, "e4m3")[:, unstriped(offs)]
    xs = unpack_weight(xs_words, xs_scales, "e4m3")
    w2 = unpack_weight(w2_words, w2_scales, "e2m1")
    wc = unpack_weight(wc_words, wc_scales, "e4m3")
    a = mxq(f64(wa), 0, "e4m3").T @ v
    b = mxq(f64(wb), 0, "e4m3").T @ xs
    h = mxq(a - b, 0, "e4m3")
    y = w2.T @ h
    e = wc.T @ xs
    return np.log(np.exp(y) + np.exp(e))

@@ -1,0 +1,243 @@
+from contextlib import ExitStack
+
+import concourse.mybir as mybir
+
+K, K2, H, N, T, S = 1536, 512, 1024, 640, 4096, 1024
+FLOPS = 2 * S * (K * H + K2 * H + H * N + K2 * N)
+
+F32 = mybir.dt.float32
+BF16 = mybir.dt.bfloat16
+I32 = mybir.dt.int32
+U32 = mybir.dt.uint32
+U16 = mybir.dt.uint16
+U8 = mybir.dt.uint8
+FP8X4 = mybir.dt.float8_e4m3fn_x4
+FP4X4 = mybir.dt.float4_e2m1fn_x4
+ALU = mybir.AluOpType
+ACT = mybir.ActivationFunctionType
+
+P = 128
+PACK = 4
+K_PASS = P * PACK
+BANK = 512
+BANKS = 8
+TAB_PASSES = K // K_PASS
+BLOCKS = H // K_PASS
+SLICES = S // P
+N_TILES = N // P
+HALVES = S // BANK
+CLAMP = 30.0
+M_SPLIT = 88
+
+
+def tile_list_cough_alert_scores_kernel(
+    tc, tab_words, tab_scales, offs, xs_words, xs_scales, wa, wb, w2_words, w2_scales, wc_words, wc_scales, out
+):
+    nc = tc.nc
+    with ExitStack() as ctx:
+        keep = ctx.enter_context(tc.tile_pool(name="keep", bufs=1))
+        wide = ctx.enter_context(tc.tile_pool(name="wide", bufs=8))
+        stage = ctx.enter_context(tc.tile_pool(name="stage", bufs=3))
+        psum = ctx.enter_context(tc.psum_pool(name="psum", bufs=1))
+
+        def bank(index):
+            return psum.tile([P, BANK], F32, name="bank%d" % (index % BANKS))
+
+        offsets = keep.tile([P, S // 16], U16, name="offsets")
+        nc.sync.dma_start(offsets[:], offs)
+
+        xs_plane = keep.tile([P, S], U8, align_bytes=64)
+        wc_plane = keep.tile([P, N], U8, align_bytes=64)
+        tab_plane = keep.tile([P, T], U8, align_bytes=64)
+        w2_plane = keep.tile([P, BLOCKS, N], U8, align_bytes=64)
+        nc.gpsimd.memset(xs_plane[:].bitcast(I32), 0)
+        nc.gpsimd.memset(wc_plane[:].bitcast(I32), 0)
+        nc.vector.memset(tab_plane[:].bitcast(I32), 0)
+        nc.vector.memset(w2_plane[:].rearrange("p a n -> p (a n)").bitcast(I32), 0)
+        def load_plane(plane, scales):
+            for q in range(4):
+                nc.sync.dma_start(
+                    plane[32 * q : 32 * q + 4].bitcast(I32),
+                    scales[:, 4 * q : 4 * q + 4, :].rearrange("a r n -> r a n").bitcast(I32),
+                )
+
+        def load_words(name, words, width):
+            tile = keep.tile([P, width], I32, name=name, align_bytes=64)
+            nc.sync.dma_start(tile[:], words.rearrange("p c i -> p (c i)").bitcast(I32))
+            return tile
+
+        def load_weight(w, a, b):
+            raw = wide.tile([P, PACK, BANK], F32, name="wide")
+            rows = w[a * K_PASS : (a + 1) * K_PASS, b * K_PASS : (b + 1) * K_PASS]
+            nc.sync.dma_start(raw[:], rows.rearrange("(p j) c -> p j c", j=PACK))
+            return raw
+
+        xs_codes = load_words("xs_codes", xs_words[0], S)
+        wc_codes = load_words("wc_codes", wc_words[0], N)
+        load_plane(xs_plane[:].rearrange("p (a n) -> p a n", a=1), xs_scales)
+        raw = {}
+        table = {}
+        raw["b", 0] = load_weight(wb, 0, 0)
+        load_plane(wc_plane[:].rearrange("p (a n) -> p a n", a=1), wc_scales)
+        table[0] = load_words("table0", tab_words[0], T)
+        for q in range(4):
+            nc.sync.dma_start(
+                tab_plane[32 * q : 32 * q + 4 * TAB_PASSES, :].bitcast(I32),
+                tab_scales[:, 4 * q : 4 * q + 4, :].bitcast(I32),
+            )
+        for a in range(TAB_PASSES):
+            raw[a, 0] = load_weight(wa, a, 0)
+        table[1] = load_words("table1", tab_words[1], T)
+        table[2] = load_words("table2", tab_words[2], T)
+        raw["b", 1] = load_weight(wb, 0, 1)
+        load_plane(w2_plane[:], w2_scales)
+        for a in range(TAB_PASSES):
+            raw[a, 1] = load_weight(wa, a, 1)
+        w2_codes = keep.tile([P, BLOCKS, 2 * N], U8, align_bytes=64)
+        nc.sync.dma_start(w2_codes[:].bitcast(I32), w2_words.rearrange("a p c -> p a c").bitcast(I32))
+
+        def quantize_weight(key, sign, m_split):
+            grouped = stage.tile([P, PACK * BANK], BF16, name="grouped", align_bytes=64)
+            dst = grouped[:].rearrange("p (t m j) -> p m j t", t=PACK, j=PACK)
+            src = raw[key][:].rearrange("p j (m t) -> p m j t", t=PACK)
+            if m_split > 0:
+                nc.vector.tensor_scalar_mul(dst[:, :m_split], src[:, :m_split], sign)
+            if m_split < P:
+                nc.scalar.activation(dst[:, m_split:], src[:, m_split:], ACT.Copy, scale=sign)
+            codes = keep.tile([P, BANK], U32, name="codes_%s_%d" % key, align_bytes=64)
+            scales = keep.tile([P, BANK], U8, name="scales_%s_%d" % key, align_bytes=64)
+            nc.vector.quantize_mx(out=codes[:].bitcast(FP8X4), scales=scales[:], in_=grouped[:])
+            return codes, scales
+
+        def cols(index, width):
+            return slice(index * width, (index + 1) * width)
+
+        def e_pass(acc, i, half, stop):
+            nc.tensor.matmul_mx(
+                out=acc[:],
+                lhsT=wc_codes[:, cols(i, P)].bitcast(FP8X4),
+                lhsT_scale=wc_plane[:, cols(i, P)],
+                rhs=xs_codes[:, cols(half, BANK)].bitcast(FP8X4),
+                rhs_scale=xs_plane[:, cols(half, BANK)],
+                start=True,
+                stop=stop,
+            )
+
+        out_tiles = [(half, i) for half in range(HALVES) for i in range(N_TILES)]
+
+        quant = {}
+        quant["b", 0] = quantize_weight(("b", 0), 1.0, 0)
+
+        e_sb = []
+        for k, (half, i) in enumerate(out_tiles):
+            acc = bank(k)
+            e_pass(acc, i, half, True)
+            tile = keep.tile([P, BANK], F32, name="e_sb%d" % k)
+            nc.scalar.copy(tile[:], acc[:])
+            e_sb.append(tile)
+
+        picked = {}
+
+        def gather_words(a, pieces):
+            tile = keep.tile([P, S], U32, name="picked%d" % a, align_bytes=64)
+            width = S // pieces
+            for c in range(pieces):
+                nc.vector.tensor_copy(tile[:, cols(c, width)], table[a][:].bitcast(U32).indirect(offsets[:, cols(c, width // 16)]))
+            picked[a] = tile
+
+        h_codes = [keep.tile([P, S], U32, name="h_codes%d" % b, align_bytes=64) for b in range(BLOCKS)]
+        h_scales = [keep.tile([P, S], U8, name="h_scales%d" % b, align_bytes=64) for b in range(BLOCKS)]
+
+        def h_pass(accs, key, first, last):
+            codes, scales = quant[key]
+            for s in range(SLICES):
+                if key[0] == "b":
+                    rhs, rhs_scale = xs_codes[:, cols(s, P)], xs_plane[:, cols(s, P)]
+                else:
+                    rhs, rhs_scale = picked[key[0]][:, cols(s, P)], picked_plane[4 * key[0] :, cols(s, P)]
+                for t in range(PACK):
+                    nc.tensor.matmul_mx(
+                        out=accs[s][:, cols(t, P)],
+                        lhsT=codes[:, cols(t, P)].bitcast(FP8X4),
+                        lhsT_scale=scales[:, cols(t, P)],
+                        rhs=rhs.bitcast(FP8X4),
+                        rhs_scale=rhs_scale,
+                        start=first and t == 0,
+                        stop=last and t == PACK - 1,
+                    )
+
+        def quantize_h(accs, b, on_vector):
+            rounded = {}
+            for s in range(SLICES + 1):
+                if s < SLICES:
+                    rounded[s] = stage.tile([P, P, PACK], BF16, name="h_rounded", align_bytes=64, bufs=SLICES)
+                    src = accs[s][:].rearrange("p (t j) -> p j t", t=PACK)
+                    if s in on_vector:
+                        nc.vector.tensor_copy(rounded[s][:], src)
+                    else:
+                        nc.scalar.copy(rounded[s][:], src)
+                if s > 0:
+                    nc.vector.quantize_mx(
+                        out=h_codes[b][:, cols(s - 1, P)].bitcast(FP8X4),
+                        scales=h_scales[b][:, cols(s - 1, P)],
+                        in_=rounded[s - 1][:].rearrange("p j t -> p (j t)"),
+                    )
+
+        accs = [bank(s) for s in range(SLICES)]
+        h_pass(accs, ("b", 0), True, False)
+        gather_words(0, 1)
+        quant[0, 0] = quantize_weight((0, 0), -1.0, P)
+        picked_plane = keep.tile([P, S], U8, align_bytes=64)
+        nc.vector.tensor_copy(picked_plane[:], tab_plane[:].indirect(offsets[:]))
+        h_pass(accs, (0, 0), False, False)
+        quant[1, 0] = quantize_weight((1, 0), -1.0, P)
+        quant[2, 0] = quantize_weight((2, 0), -1.0, 0)
+        gather_words(1, HALVES)
+        h_pass(accs, (1, 0), False, False)
+        gather_words(2, HALVES)
+        h_pass(accs, (2, 0), False, True)
+        quant["b", 1] = quantize_weight(("b", 1), 1.0, P)
+        quantize_h(accs, 0, ())
+
+        accs = [bank(s) for s in range(SLICES)]
+        h_pass(accs, ("b", 1), True, False)
+        quant[0, 1] = quantize_weight((0, 1), -1.0, P)
+        h_pass(accs, (0, 1), False, False)
+        quant[1, 1] = quantize_weight((1, 1), -1.0, M_SPLIT)
+        h_pass(accs, (1, 1), False, False)
+        quant[2, 1] = quantize_weight((2, 1), -1.0, M_SPLIT)
+        h_pass(accs, (2, 1), False, True)
+        quantize_h(accs, 1, (1, 3))
+
+        work = [wide.tile([P, 2 * S], F32, name="wide") for i in range(N_TILES)]
+        gap = [work[i][:, cols(half, BANK)] for half, i in out_tiles]
+        grown = [work[i][:, cols(HALVES + half, BANK)] for half, i in out_tiles]
+        for k, (half, i) in enumerate(out_tiles):
+            acc = bank(k)
+            in_psum = k > 0
+            if in_psum:
+                e_pass(acc, i, half, False)
+            for b in range(BLOCKS):
+                nc.tensor.matmul_mx(
+                    out=acc[:],
+                    lhsT=w2_codes[:, b, cols(i, 2 * P)].bitcast(FP4X4),
+                    lhsT_scale=w2_plane[:, b, cols(i, P)],
+                    rhs=h_codes[b][:, cols(half, BANK)].bitcast(FP8X4),
+                    rhs_scale=h_scales[b][:, cols(half, BANK)],
+                    start=(b == 0 and not in_psum),
+                    stop=(b == BLOCKS - 1),
+                )
+            if in_psum:
+                nc.vector.tensor_scalar_min(gap[k], acc[:], CLAMP)
+            else:
+                nc.vector.tensor_tensor(gap[k], acc[:], e_sb[k][:], ALU.add)
+                nc.vector.tensor_scalar_min(gap[k], gap[k], CLAMP)
+            nc.scalar.activation(grown[k], gap[k], ACT.Exp)
+        one = keep.tile([P, 1], F32)
+        nc.scalar.activation(one[:], grown[-1][:, 0:1], ACT.Copy, scale=0.0, bias=1.0)
+        for k in range(len(out_tiles)):
+            nc.vector.tensor_tensor(e_sb[k][:], gap[k], e_sb[k][:], ALU.subtract)
+        for k, (half, i) in enumerate(out_tiles):
+            nc.scalar.activation(grown[k], grown[k], ACT.Ln, bias=one[:])
+            nc.vector.tensor_tensor(gap[k], grown[k], e_sb[k][:], ALU.subtract)
+            nc.sync.dma_start(out[cols(i, P), cols(half, BANK)], gap[k])

@@ -1,3 +1,4 @@
+import math
 from contextlib import ExitStack
 
 import concourse.mybir as mybir
@@ -27,7 +28,8 @@ SLICES = S // P
 N_TILES = N // P
 HALVES = S // BANK
 CLAMP = 30.0
-M_SPLIT = 88
+M_SPLIT = 48
+AHEAD = 2
 
 
 def tile_list_cough_alert_scores_kernel(
@@ -36,9 +38,12 @@ def tile_list_cough_alert_scores_kernel(
     nc = tc.nc
     with ExitStack() as ctx:
         keep = ctx.enter_context(tc.tile_pool(name="keep", bufs=1))
-        wide = ctx.enter_context(tc.tile_pool(name="wide", bufs=8))
+        wide = ctx.enter_context(tc.tile_pool(name="wide", bufs=6))
         stage = ctx.enter_context(tc.tile_pool(name="stage", bufs=3))
         psum = ctx.enter_context(tc.psum_pool(name="psum", bufs=1))
+
+        def cols(index, width):
+            return slice(index * width, (index + 1) * width)
 
         def bank(index):
             return psum.tile([P, BANK], F32, name="bank%d" % (index % BANKS))
@@ -54,6 +59,12 @@ def tile_list_cough_alert_scores_kernel(
         nc.gpsimd.memset(wc_plane[:].bitcast(I32), 0)
         nc.vector.memset(tab_plane[:].bitcast(I32), 0)
         nc.vector.memset(w2_plane[:].rearrange("p a n -> p (a n)").bitcast(I32), 0)
+        for q in range(4):
+            nc.gpsimd.dma_start(
+                tab_plane[32 * q + 4 : 32 * q + 4 + 4 * TAB_PASSES, :].bitcast(I32),
+                tab_scales[:, 4 * q : 4 * q + 4, :].bitcast(I32),
+            )
+
         def load_plane(plane, scales):
             for q in range(4):
                 nc.sync.dma_start(
@@ -66,10 +77,11 @@ def tile_list_cough_alert_scores_kernel(
             nc.sync.dma_start(tile[:], words.rearrange("p c i -> p (c i)").bitcast(I32))
             return tile
 
-        def load_weight(w, a, b):
-            raw = wide.tile([P, PACK, BANK], F32, name="wide")
+        def load_weight(w, a, b, pieces=1, pool=wide, name="wide"):
+            raw = pool.tile([P, pieces, PACK, BANK // pieces], F32, name=name, align_bytes=64)
             rows = w[a * K_PASS : (a + 1) * K_PASS, b * K_PASS : (b + 1) * K_PASS]
-            nc.sync.dma_start(raw[:], rows.rearrange("(p j) c -> p j c", j=PACK))
+            for c in range(pieces):
+                nc.sync.dma_start(raw[:, c], rows[:, cols(c, BANK // pieces)].rearrange("(p j) c -> p j c", j=PACK))
             return raw
 
         xs_codes = load_words("xs_codes", xs_words[0], S)
@@ -80,37 +92,41 @@ def tile_list_cough_alert_scores_kernel(
         raw["b", 0] = load_weight(wb, 0, 0)
         load_plane(wc_plane[:].rearrange("p (a n) -> p a n", a=1), wc_scales)
         table[0] = load_words("table0", tab_words[0], T)
-        for q in range(4):
-            nc.sync.dma_start(
-                tab_plane[32 * q : 32 * q + 4 * TAB_PASSES, :].bitcast(I32),
-                tab_scales[:, 4 * q : 4 * q + 4, :].bitcast(I32),
-            )
-        for a in range(TAB_PASSES):
-            raw[a, 0] = load_weight(wa, a, 0)
+        raw[0, 0] = load_weight(wa, 0, 0)
+        raw[1, 0] = load_weight(wa, 1, 0)
+        raw[2, 0] = load_weight(wa, 2, 0)
         table[1] = load_words("table1", tab_words[1], T)
         table[2] = load_words("table2", tab_words[2], T)
-        raw["b", 1] = load_weight(wb, 0, 1)
+        raw["b", 1] = load_weight(wb, 0, 1, 2)
         load_plane(w2_plane[:], w2_scales)
-        for a in range(TAB_PASSES):
-            raw[a, 1] = load_weight(wa, a, 1)
+        raw[0, 1] = load_weight(wa, 0, 1, pool=keep, name="then_h0")
+        raw[1, 1] = load_weight(wa, 1, 1)
+        raw[2, 1] = load_weight(wa, 2, 1, pool=keep, name="then_h1")
         w2_codes = keep.tile([P, BLOCKS, 2 * N], U8, align_bytes=64)
         nc.sync.dma_start(w2_codes[:].bitcast(I32), w2_words.rearrange("a p c -> p a c").bitcast(I32))
 
-        def quantize_weight(key, sign, m_split):
+        def quantize_weight(key, sign, m_split, parts=1):
             grouped = stage.tile([P, PACK * BANK], BF16, name="grouped", align_bytes=64)
-            dst = grouped[:].rearrange("p (t m j) -> p m j t", t=PACK, j=PACK)
-            src = raw[key][:].rearrange("p j (m t) -> p m j t", t=PACK)
-            if m_split > 0:
-                nc.vector.tensor_scalar_mul(dst[:, :m_split], src[:, :m_split], sign)
-            if m_split < P:
-                nc.scalar.activation(dst[:, m_split:], src[:, m_split:], ACT.Copy, scale=sign)
+            pieces = raw[key].shape[1]
+            for c in range(pieces):
+                for pair in range(PACK // 2):
+                    dst = grouped[:].rearrange("p (t m j) -> p m j t", t=PACK, j=PACK)[:, cols(c, P // pieces), :, cols(pair, 2)]
+                    src = raw[key][:, c].rearrange("p j (m t) -> p m j t", t=PACK)[:, :, :, cols(pair, 2)]
+                    m = m_split[pair]
+                    if m > 0:
+                        nc.vector.tensor_scalar_mul(dst[:, :m], src[:, :m], sign)
+                    if m < P // pieces:
+                        nc.scalar.activation(dst[:, m:], src[:, m:], ACT.Copy, scale=sign)
             codes = keep.tile([P, BANK], U32, name="codes_%s_%d" % key, align_bytes=64)
             scales = keep.tile([P, BANK], U8, name="scales_%s_%d" % key, align_bytes=64)
-            nc.vector.quantize_mx(out=codes[:].bitcast(FP8X4), scales=scales[:], in_=grouped[:])
+            width = BANK // parts
+            for c in range(parts):
+                nc.vector.quantize_mx(
+                    out=codes[:, cols(c, width)].bitcast(FP8X4),
+                    scales=scales[:, cols(c, width)],
+                    in_=grouped[:, cols(c, PACK * width)],
+                )
             return codes, scales
-
-        def cols(index, width):
-            return slice(index * width, (index + 1) * width)
 
         def e_pass(acc, i, half, stop):
             nc.tensor.matmul_mx(
@@ -126,7 +142,7 @@ def tile_list_cough_alert_scores_kernel(
         out_tiles = [(half, i) for half in range(HALVES) for i in range(N_TILES)]
 
         quant = {}
-        quant["b", 0] = quantize_weight(("b", 0), 1.0, 0)
+        quant["b", 0] = quantize_weight(("b", 0), 1.0, (0, 0), 2)
 
         e_sb = []
         for k, (half, i) in enumerate(out_tiles):
@@ -145,8 +161,9 @@ def tile_list_cough_alert_scores_kernel(
                 nc.vector.tensor_copy(tile[:, cols(c, width)], table[a][:].bitcast(U32).indirect(offsets[:, cols(c, width // 16)]))
             picked[a] = tile
 
-        h_codes = [keep.tile([P, S], U32, name="h_codes%d" % b, align_bytes=64) for b in range(BLOCKS)]
-        h_scales = [keep.tile([P, S], U8, name="h_scales%d" % b, align_bytes=64) for b in range(BLOCKS)]
+        h_codes = {}
+        h_scales = {}
+        rounded = {}
 
         def h_pass(accs, key, first, last):
             codes, scales = quant[key]
@@ -154,7 +171,7 @@ def tile_list_cough_alert_scores_kernel(
                 if key[0] == "b":
                     rhs, rhs_scale = xs_codes[:, cols(s, P)], xs_plane[:, cols(s, P)]
                 else:
-                    rhs, rhs_scale = picked[key[0]][:, cols(s, P)], picked_plane[4 * key[0] :, cols(s, P)]
+                    rhs, rhs_scale = picked[key[0]][:, cols(s, P)], picked_plane[4 + 4 * key[0] :, cols(s, P)]
                 for t in range(PACK):
                     nc.tensor.matmul_mx(
                         out=accs[s][:, cols(t, P)],
@@ -166,78 +183,102 @@ def tile_list_cough_alert_scores_kernel(
                         stop=last and t == PACK - 1,
                     )
 
-        def quantize_h(accs, b, on_vector):
-            rounded = {}
-            for s in range(SLICES + 1):
-                if s < SLICES:
-                    rounded[s] = stage.tile([P, P, PACK], BF16, name="h_rounded", align_bytes=64, bufs=SLICES)
-                    src = accs[s][:].rearrange("p (t j) -> p j t", t=PACK)
-                    if s in on_vector:
-                        nc.vector.tensor_copy(rounded[s][:], src)
-                    else:
-                        nc.scalar.copy(rounded[s][:], src)
-                if s > 0:
-                    nc.vector.quantize_mx(
-                        out=h_codes[b][:, cols(s - 1, P)].bitcast(FP8X4),
-                        scales=h_scales[b][:, cols(s - 1, P)],
-                        in_=rounded[s - 1][:].rearrange("p j t -> p (j t)"),
-                    )
+        def round_h(accs, b, on_vector):
+            for half in range(HALVES):
+                rounded[b, half] = keep.tile([P, BANK, PACK], BF16, name="rounded%d%d" % (b, half), align_bytes=64)
+            for s in range(SLICES):
+                half, within = divmod(s, SLICES // HALVES)
+                dst = rounded[b, half][:, cols(within, P)]
+                src = accs[s][:].rearrange("p (t j) -> p j t", t=PACK)
+                if s in on_vector:
+                    nc.vector.tensor_copy(dst, src)
+                else:
+                    nc.scalar.copy(dst, src)
+
+        def quantize_h(b, half, name, parts):
+            h_codes[b, half] = keep.tile([P, BANK], U32, name=name, align_bytes=64)
+            h_scales[b, half] = keep.tile([P, BANK], U8, name="h_scales%d%d" % (b, half), align_bytes=64)
+            width = BANK // parts
+            for c in range(parts):
+                nc.vector.quantize_mx(
+                    out=h_codes[b, half][:, cols(c, width)].bitcast(FP8X4),
+                    scales=h_scales[b, half][:, cols(c, width)],
+                    in_=rounded[b, half][:, cols(c, width)].rearrange("p j t -> p (j t)"),
+                )
 
         accs = [bank(s) for s in range(SLICES)]
         h_pass(accs, ("b", 0), True, False)
         gather_words(0, 1)
-        quant[0, 0] = quantize_weight((0, 0), -1.0, P)
+        quant[0, 0] = quantize_weight((0, 0), -1.0, (P, P), 2)
         picked_plane = keep.tile([P, S], U8, align_bytes=64)
         nc.vector.tensor_copy(picked_plane[:], tab_plane[:].indirect(offsets[:]))
         h_pass(accs, (0, 0), False, False)
-        quant[1, 0] = quantize_weight((1, 0), -1.0, P)
-        quant[2, 0] = quantize_weight((2, 0), -1.0, 0)
+        quant[1, 0] = quantize_weight((1, 0), -1.0, (P, P), 2)
+        quant[2, 0] = quantize_weight((2, 0), -1.0, (0, 0), 2)
         gather_words(1, HALVES)
         h_pass(accs, (1, 0), False, False)
         gather_words(2, HALVES)
         h_pass(accs, (2, 0), False, True)
-        quant["b", 1] = quantize_weight(("b", 1), 1.0, P)
-        quantize_h(accs, 0, ())
+        quant["b", 1] = quantize_weight(("b", 1), 1.0, (P // 2, P // 2), 2)
+        round_h(accs, 0, (6,))
 
         accs = [bank(s) for s in range(SLICES)]
         h_pass(accs, ("b", 1), True, False)
-        quant[0, 1] = quantize_weight((0, 1), -1.0, P)
+        quant[0, 1] = quantize_weight((0, 1), -1.0, (P, P), 2)
         h_pass(accs, (0, 1), False, False)
-        quant[1, 1] = quantize_weight((1, 1), -1.0, M_SPLIT)
+        quantize_h(0, 0, "then_h0", 1)
+        quant[1, 1] = quantize_weight((1, 1), -1.0, (P, M_SPLIT), 2)
         h_pass(accs, (1, 1), False, False)
-        quant[2, 1] = quantize_weight((2, 1), -1.0, M_SPLIT)
+        quant[2, 1] = quantize_weight((2, 1), -1.0, (P, M_SPLIT), 2)
         h_pass(accs, (2, 1), False, True)
-        quantize_h(accs, 1, (1, 3))
+        quantize_h(0, 1, "then_h1", 1)
+        round_h(accs, 1, (1, 3))
+        quantize_h(1, 0, "h_codes10", 2)
+        quantize_h(1, 1, "h_codes11", 1)
 
-        work = [wide.tile([P, 2 * S], F32, name="wide") for i in range(N_TILES)]
-        gap = [work[i][:, cols(half, BANK)] for half, i in out_tiles]
-        grown = [work[i][:, cols(HALVES + half, BANK)] for half, i in out_tiles]
-        for k, (half, i) in enumerate(out_tiles):
-            acc = bank(k)
-            in_psum = k > 0
-            if in_psum:
-                e_pass(acc, i, half, False)
-            for b in range(BLOCKS):
-                nc.tensor.matmul_mx(
-                    out=acc[:],
-                    lhsT=w2_codes[:, b, cols(i, 2 * P)].bitcast(FP4X4),
-                    lhsT_scale=w2_plane[:, b, cols(i, P)],
-                    rhs=h_codes[b][:, cols(half, BANK)].bitcast(FP8X4),
-                    rhs_scale=h_scales[b][:, cols(half, BANK)],
-                    start=(b == 0 and not in_psum),
-                    stop=(b == BLOCKS - 1),
-                )
-            if in_psum:
-                nc.vector.tensor_scalar_min(gap[k], acc[:], CLAMP)
-            else:
-                nc.vector.tensor_tensor(gap[k], acc[:], e_sb[k][:], ALU.add)
-                nc.vector.tensor_scalar_min(gap[k], gap[k], CLAMP)
-            nc.scalar.activation(grown[k], gap[k], ACT.Exp)
+        work = [wide.tile([P, 2 * S], F32, name="wide", align_bytes=64) for i in range(N_TILES)]
+        grown = [work[i][:, cols(half, BANK)] for half, i in out_tiles]
+        result = [work[i][:, cols(HALVES + half, BANK)] for half, i in out_tiles]
+        accs = {}
         one = keep.tile([P, 1], F32)
-        nc.scalar.activation(one[:], grown[-1][:, 0:1], ACT.Copy, scale=0.0, bias=1.0)
-        for k in range(len(out_tiles)):
-            nc.vector.tensor_tensor(e_sb[k][:], gap[k], e_sb[k][:], ALU.subtract)
+
+        def y_pass(k, b, start):
+            half, i = out_tiles[k]
+            nc.tensor.matmul_mx(
+                out=accs[k][:],
+                lhsT=w2_codes[:, b, cols(i, 2 * P)].bitcast(FP4X4),
+                lhsT_scale=w2_plane[:, b, cols(i, P)],
+                rhs=h_codes[b, half][:].bitcast(FP8X4),
+                rhs_scale=h_scales[b, half][:],
+                start=start,
+                stop=(b == BLOCKS - 1),
+            )
+
+        def open_tile(k):
+            half, i = out_tiles[k]
+            accs[k] = bank(k)
+            if k > 0:
+                e_pass(accs[k], i, half, False)
+            y_pass(k, 0, k == 0)
+
+        def close_tile(k):
+            y_pass(k, 1, False)
+            gap = accs[k][:]
+            if k == 0:
+                nc.vector.tensor_tensor(result[k], gap, e_sb[k][:], ALU.add)
+                gap = result[k]
+            nc.scalar.activation(grown[k], gap, ACT.Exp)
+            if k == len(out_tiles) - 1:
+                nc.scalar.activation(one[:], gap[:, 0:1], ACT.Copy, scale=0.0, bias=1.0)
+            nc.vector.scalar_tensor_tensor(e_sb[k][:], gap, CLAMP, e_sb[k][:], ALU.min, ALU.subtract)
+            nc.vector.tensor_scalar_min(grown[k], grown[k], math.exp(CLAMP))
+
+        for k in range(len(out_tiles) + AHEAD):
+            if k < len(out_tiles):
+                open_tile(k)
+            if k >= AHEAD:
+                close_tile(k - AHEAD)
         for k, (half, i) in enumerate(out_tiles):
             nc.scalar.activation(grown[k], grown[k], ACT.Ln, bias=one[:])
-            nc.vector.tensor_tensor(gap[k], grown[k], e_sb[k][:], ALU.subtract)
-            nc.sync.dma_start(out[cols(i, P), cols(half, BANK)], gap[k])
+            nc.vector.tensor_tensor(result[k], grown[k], e_sb[k][:], ALU.subtract)
+            nc.sync.dma_start(out[cols(i, P), cols(half, BANK)], result[k])

import math
from contextlib import ExitStack

import concourse.mybir as mybir

K, K2, H, N, T, S = 1536, 512, 1024, 640, 4096, 1024
FLOPS = 2 * S * (K * H + K2 * H + H * N + K2 * N)

F32 = mybir.dt.float32
BF16 = mybir.dt.bfloat16
I32 = mybir.dt.int32
U32 = mybir.dt.uint32
U16 = mybir.dt.uint16
U8 = mybir.dt.uint8
FP8X4 = mybir.dt.float8_e4m3fn_x4
FP4X4 = mybir.dt.float4_e2m1fn_x4
ALU = mybir.AluOpType
ACT = mybir.ActivationFunctionType

P = 128
PACK = 4
K_PASS = P * PACK
BANK = 512
BANKS = 8
TAB_PASSES = K // K_PASS
BLOCKS = H // K_PASS
SLICES = S // P
N_TILES = N // P
HALVES = S // BANK
CLAMP = 30.0
M_SPLIT = 48
AHEAD = 2


def tile_list_cough_alert_scores_kernel(
    tc, tab_words, tab_scales, offs, xs_words, xs_scales, wa, wb, w2_words, w2_scales, wc_words, wc_scales, out
):
    nc = tc.nc
    with ExitStack() as ctx:
        keep = ctx.enter_context(tc.tile_pool(name="keep", bufs=1))
        wide = ctx.enter_context(tc.tile_pool(name="wide", bufs=6))
        stage = ctx.enter_context(tc.tile_pool(name="stage", bufs=3))
        psum = ctx.enter_context(tc.psum_pool(name="psum", bufs=1))

        def cols(index, width):
            return slice(index * width, (index + 1) * width)

        def bank(index):
            return psum.tile([P, BANK], F32, name="bank%d" % (index % BANKS))

        offsets = keep.tile([P, S // 16], U16, name="offsets")
        nc.sync.dma_start(offsets[:], offs)

        xs_plane = keep.tile([P, S], U8, align_bytes=64)
        wc_plane = keep.tile([P, N], U8, align_bytes=64)
        tab_plane = keep.tile([P, T], U8, align_bytes=64)
        w2_plane = keep.tile([P, BLOCKS, N], U8, align_bytes=64)
        nc.gpsimd.memset(xs_plane[:].bitcast(I32), 0)
        nc.gpsimd.memset(wc_plane[:].bitcast(I32), 0)
        nc.vector.memset(tab_plane[:].bitcast(I32), 0)
        nc.vector.memset(w2_plane[:].rearrange("p a n -> p (a n)").bitcast(I32), 0)
        for q in range(4):
            nc.gpsimd.dma_start(
                tab_plane[32 * q + 4 : 32 * q + 4 + 4 * TAB_PASSES, :].bitcast(I32),
                tab_scales[:, 4 * q : 4 * q + 4, :].bitcast(I32),
            )

        def load_plane(plane, scales):
            for q in range(4):
                nc.sync.dma_start(
                    plane[32 * q : 32 * q + 4].bitcast(I32),
                    scales[:, 4 * q : 4 * q + 4, :].rearrange("a r n -> r a n").bitcast(I32),
                )

        def load_words(name, words, width):
            tile = keep.tile([P, width], I32, name=name, align_bytes=64)
            nc.sync.dma_start(tile[:], words.rearrange("p c i -> p (c i)").bitcast(I32))
            return tile

        def load_weight(w, a, b, pieces=1, pool=wide, name="wide"):
            raw = pool.tile([P, pieces, PACK, BANK // pieces], F32, name=name, align_bytes=64)
            rows = w[a * K_PASS : (a + 1) * K_PASS, b * K_PASS : (b + 1) * K_PASS]
            for c in range(pieces):
                nc.sync.dma_start(raw[:, c], rows[:, cols(c, BANK // pieces)].rearrange("(p j) c -> p j c", j=PACK))
            return raw

        xs_codes = load_words("xs_codes", xs_words[0], S)
        wc_codes = load_words("wc_codes", wc_words[0], N)
        load_plane(xs_plane[:].rearrange("p (a n) -> p a n", a=1), xs_scales)
        raw = {}
        table = {}
        raw["b", 0] = load_weight(wb, 0, 0)
        load_plane(wc_plane[:].rearrange("p (a n) -> p a n", a=1), wc_scales)
        table[0] = load_words("table0", tab_words[0], T)
        raw[0, 0] = load_weight(wa, 0, 0)
        raw[1, 0] = load_weight(wa, 1, 0)
        raw[2, 0] = load_weight(wa, 2, 0)
        table[1] = load_words("table1", tab_words[1], T)
        table[2] = load_words("table2", tab_words[2], T)
        raw["b", 1] = load_weight(wb, 0, 1, 2)
        load_plane(w2_plane[:], w2_scales)
        raw[0, 1] = load_weight(wa, 0, 1, pool=keep, name="then_h0")
        raw[1, 1] = load_weight(wa, 1, 1)
        raw[2, 1] = load_weight(wa, 2, 1, pool=keep, name="then_h1")
        w2_codes = keep.tile([P, BLOCKS, 2 * N], U8, align_bytes=64)
        nc.sync.dma_start(w2_codes[:].bitcast(I32), w2_words.rearrange("a p c -> p a c").bitcast(I32))

        def quantize_weight(key, sign, m_split, parts=1):
            grouped = stage.tile([P, PACK * BANK], BF16, name="grouped", align_bytes=64)
            pieces = raw[key].shape[1]
            for c in range(pieces):
                for pair in range(PACK // 2):
                    dst = grouped[:].rearrange("p (t m j) -> p m j t", t=PACK, j=PACK)[:, cols(c, P // pieces), :, cols(pair, 2)]
                    src = raw[key][:, c].rearrange("p j (m t) -> p m j t", t=PACK)[:, :, :, cols(pair, 2)]
                    m = m_split[pair]
                    if m > 0:
                        nc.vector.tensor_scalar_mul(dst[:, :m], src[:, :m], sign)
                    if m < P // pieces:
                        nc.scalar.activation(dst[:, m:], src[:, m:], ACT.Copy, scale=sign)
            codes = keep.tile([P, BANK], U32, name="codes_%s_%d" % key, align_bytes=64)
            scales = keep.tile([P, BANK], U8, name="scales_%s_%d" % key, align_bytes=64)
            width = BANK // parts
            for c in range(parts):
                nc.vector.quantize_mx(
                    out=codes[:, cols(c, width)].bitcast(FP8X4),
                    scales=scales[:, cols(c, width)],
                    in_=grouped[:, cols(c, PACK * width)],
                )
            return codes, scales

        def e_pass(acc, i, half, stop):
            nc.tensor.matmul_mx(
                out=acc[:],
                lhsT=wc_codes[:, cols(i, P)].bitcast(FP8X4),
                lhsT_scale=wc_plane[:, cols(i, P)],
                rhs=xs_codes[:, cols(half, BANK)].bitcast(FP8X4),
                rhs_scale=xs_plane[:, cols(half, BANK)],
                start=True,
                stop=stop,
            )

        out_tiles = [(half, i) for half in range(HALVES) for i in range(N_TILES)]

        quant = {}
        quant["b", 0] = quantize_weight(("b", 0), 1.0, (0, 0), 2)

        e_sb = []
        for k, (half, i) in enumerate(out_tiles):
            acc = bank(k)
            e_pass(acc, i, half, True)
            tile = keep.tile([P, BANK], F32, name="e_sb%d" % k)
            nc.scalar.copy(tile[:], acc[:])
            e_sb.append(tile)

        picked = {}

        def gather_words(a, pieces):
            tile = keep.tile([P, S], U32, name="picked%d" % a, align_bytes=64)
            width = S // pieces
            for c in range(pieces):
                nc.vector.tensor_copy(tile[:, cols(c, width)], table[a][:].bitcast(U32).indirect(offsets[:, cols(c, width // 16)]))
            picked[a] = tile

        h_codes = {}
        h_scales = {}
        rounded = {}

        def h_pass(accs, key, first, last):
            codes, scales = quant[key]
            for s in range(SLICES):
                if key[0] == "b":
                    rhs, rhs_scale = xs_codes[:, cols(s, P)], xs_plane[:, cols(s, P)]
                else:
                    rhs, rhs_scale = picked[key[0]][:, cols(s, P)], picked_plane[4 + 4 * key[0] :, cols(s, P)]
                for t in range(PACK):
                    nc.tensor.matmul_mx(
                        out=accs[s][:, cols(t, P)],
                        lhsT=codes[:, cols(t, P)].bitcast(FP8X4),
                        lhsT_scale=scales[:, cols(t, P)],
                        rhs=rhs.bitcast(FP8X4),
                        rhs_scale=rhs_scale,
                        start=first and t == 0,
                        stop=last and t == PACK - 1,
                    )

        def round_h(accs, b, on_vector):
            for half in range(HALVES):
                rounded[b, half] = keep.tile([P, BANK, PACK], BF16, name="rounded%d%d" % (b, half), align_bytes=64)
            for s in range(SLICES):
                half, within = divmod(s, SLICES // HALVES)
                dst = rounded[b, half][:, cols(within, P)]
                src = accs[s][:].rearrange("p (t j) -> p j t", t=PACK)
                if s in on_vector:
                    nc.vector.tensor_copy(dst, src)
                else:
                    nc.scalar.copy(dst, src)

        def quantize_h(b, half, name, parts):
            h_codes[b, half] = keep.tile([P, BANK], U32, name=name, align_bytes=64)
            h_scales[b, half] = keep.tile([P, BANK], U8, name="h_scales%d%d" % (b, half), align_bytes=64)
            width = BANK // parts
            for c in range(parts):
                nc.vector.quantize_mx(
                    out=h_codes[b, half][:, cols(c, width)].bitcast(FP8X4),
                    scales=h_scales[b, half][:, cols(c, width)],
                    in_=rounded[b, half][:, cols(c, width)].rearrange("p j t -> p (j t)"),
                )

        accs = [bank(s) for s in range(SLICES)]
        h_pass(accs, ("b", 0), True, False)
        gather_words(0, 1)
        quant[0, 0] = quantize_weight((0, 0), -1.0, (P, P), 2)
        picked_plane = keep.tile([P, S], U8, align_bytes=64)
        nc.vector.tensor_copy(picked_plane[:], tab_plane[:].indirect(offsets[:]))
        h_pass(accs, (0, 0), False, False)
        quant[1, 0] = quantize_weight((1, 0), -1.0, (P, P), 2)
        quant[2, 0] = quantize_weight((2, 0), -1.0, (0, 0), 2)
        gather_words(1, HALVES)
        h_pass(accs, (1, 0), False, False)
        gather_words(2, HALVES)
        h_pass(accs, (2, 0), False, True)
        quant["b", 1] = quantize_weight(("b", 1), 1.0, (P // 2, P // 2), 2)
        round_h(accs, 0, (6,))

        accs = [bank(s) for s in range(SLICES)]
        h_pass(accs, ("b", 1), True, False)
        quant[0, 1] = quantize_weight((0, 1), -1.0, (P, P), 2)
        h_pass(accs, (0, 1), False, False)
        quantize_h(0, 0, "then_h0", 1)
        quant[1, 1] = quantize_weight((1, 1), -1.0, (P, M_SPLIT), 2)
        h_pass(accs, (1, 1), False, False)
        quant[2, 1] = quantize_weight((2, 1), -1.0, (P, M_SPLIT), 2)
        h_pass(accs, (2, 1), False, True)
        quantize_h(0, 1, "then_h1", 1)
        round_h(accs, 1, (1, 3))
        quantize_h(1, 0, "h_codes10", 2)
        quantize_h(1, 1, "h_codes11", 1)

        work = [wide.tile([P, 2 * S], F32, name="wide", align_bytes=64) for i in range(N_TILES)]
        grown = [work[i][:, cols(half, BANK)] for half, i in out_tiles]
        result = [work[i][:, cols(HALVES + half, BANK)] for half, i in out_tiles]
        accs = {}
        one = keep.tile([P, 1], F32)

        def y_pass(k, b, start):
            half, i = out_tiles[k]
            nc.tensor.matmul_mx(
                out=accs[k][:],
                lhsT=w2_codes[:, b, cols(i, 2 * P)].bitcast(FP4X4),
                lhsT_scale=w2_plane[:, b, cols(i, P)],
                rhs=h_codes[b, half][:].bitcast(FP8X4),
                rhs_scale=h_scales[b, half][:],
                start=start,
                stop=(b == BLOCKS - 1),
            )

        def open_tile(k):
            half, i = out_tiles[k]
            accs[k] = bank(k)
            if k > 0:
                e_pass(accs[k], i, half, False)
            y_pass(k, 0, k == 0)

        def close_tile(k):
            y_pass(k, 1, False)
            gap = accs[k][:]
            if k == 0:
                nc.vector.tensor_tensor(result[k], gap, e_sb[k][:], ALU.add)
                gap = result[k]
            nc.scalar.activation(grown[k], gap, ACT.Exp)
            if k == len(out_tiles) - 1:
                nc.scalar.activation(one[:], gap[:, 0:1], ACT.Copy, scale=0.0, bias=1.0)
            nc.vector.scalar_tensor_tensor(e_sb[k][:], gap, CLAMP, e_sb[k][:], ALU.min, ALU.subtract)
            nc.vector.tensor_scalar_min(grown[k], grown[k], math.exp(CLAMP))

        for k in range(len(out_tiles) + AHEAD):
            if k < len(out_tiles):
                open_tile(k)
            if k >= AHEAD:
                close_tile(k - AHEAD)
        for k, (half, i) in enumerate(out_tiles):
            nc.scalar.activation(grown[k], grown[k], ACT.Ln, bias=one[:])
            nc.vector.tensor_tensor(result[k], grown[k], e_sb[k][:], ALU.subtract)
            nc.sync.dma_start(out[cols(i, P), cols(half, BANK)], result[k])
